import numpy as np
import ml_dtypes


def mxq(x, axis, fmt="e4m3"):
    dtype, down = {"e4m3": (ml_dtypes.float8_e4m3fn, 7), "e5m2": (ml_dtypes.float8_e5m2, 14)}[fmt]
    v = np.moveaxis(np.asarray(x, np.float32).astype(ml_dtypes.bfloat16).astype(np.float64), axis, -1)
    blocks = v.reshape(v.shape[:-1] + (-1, 32))
    amax = np.abs(blocks).max(-1, keepdims=True)
    byte = np.maximum(np.where(amax > 0, np.frexp(amax)[1] - 1 + 127, 0) - down, 1)
    scale = np.exp2(byte - 127.0)
    codes = (blocks / scale).astype(np.float32).astype(dtype).astype(np.float64)
    return np.moveaxis((codes * scale).reshape(v.shape), -1, axis)


WIDE = False


def mx_kscale(k):
    if not WIDE:
        return np.ones(k)
    levels = np.array([10, -10, 5, -5, 0])
    if k % 512:
        return np.exp2(np.random.permutation(np.resize(levels, k // 32))).repeat(32)
    a = np.empty((k // 512, 16))
    for p in range(k // 512):
        a[p, :8] = np.random.permutation(np.resize(levels, 8))
        for g in range(8):
            far = levels[np.abs(levels - a[p, g]) >= 10]
            a[p, g + 8] = far[np.random.randint(len(far))]
    return np.exp2(a.ravel()).repeat(32)


def f64(x):
    return np.asarray(x).astype(np.float64)


def striped(idx):
    return np.tile(np.asarray(idx).reshape(-1, 16).T, (8, 1)).astype(np.uint16)


def unstriped(offs):
    return offs[:16].T.reshape(-1).astype(np.int64)


E2M1 = np.array([0.0, 0.5, 1.0, 1.5, 2.0, 3.0, 4.0, 6.0, -0.0, -0.5, -1.0, -1.5, -2.0, -3.0, -4.0, -6.0])


def pack_weight(w, fmt):
    k, n = w.shape
    w = f64(np.asarray(w, np.float32).astype(ml_dtypes.bfloat16)).reshape(k // 32, 32, n)
    amax = np.abs(w).max(1)
    if fmt == "e4m3":
        byte = np.frexp(amax)[1] - 1 + 127 - 7
    else:
        mant, ex = np.frexp(amax / 6.0)
        byte = np.where(mant > 0.5, ex, ex - 1) + 127
    byte = np.clip(np.where(amax > 0, byte, 1), 1, 254)
    scaled = (w * np.exp2(127.0 - byte)[:, None, :]).reshape(k, n).astype(np.float32)
    by_word = np.ascontiguousarray(scaled.reshape(k // 512, 128, 4, n).transpose(0, 1, 3, 2))
    if fmt == "e4m3":
        words = by_word.astype(ml_dtypes.float8_e4m3fn).view(np.uint8)
    else:
        c = by_word.astype(ml_dtypes.float4_e2m1fn).view(np.uint8) & 0xF
        words = (c[..., 0::2] | (c[..., 1::2] << 4)).reshape(k // 512, 128, 2 * n)
    return np.ascontiguousarray(words), np.ascontiguousarray(byte.astype(np.uint8).reshape(k // 512, 16, n))


def unpack_weight(words, scales, fmt):
    g, _, n = scales.shape
    words = np.ascontiguousarray(words).reshape(g, 128, n, -1)
    if fmt == "e4m3":
        vals = words.view(ml_dtypes.float8_e4m3fn).astype(np.float64)
    else:
        nib = np.empty((g, 128, n, 4), np.uint8)
        nib[..., 0::2] = words & 0xF
        nib[..., 1::2] = words >> 4
        vals = E2M1[nib]
    vals = vals * np.repeat(np.exp2(scales.astype(np.float64) - 127.0), 8, axis=1)[..., None]
    return vals.transpose(0, 1, 3, 2).reshape(g * 512, n)


K, T, J, I, R, N = 512, 2048, 1024, 512, 512, 512


def setup_inputs():
    n = np.random.standard_normal
    idx = np.random.permutation(T)[:J]
    fk = mx_kscale(K)
    fr = mx_kscale(R)
    xtp = pack_weight(n((K, T)) / fk[:, None], "e4m3")
    wap = pack_weight(n((K, R)) * 1 / np.sqrt(K) * fk[:, None] * fr, "e2m1")
    wbp = pack_weight(n((R, N)) * 1 / np.sqrt(R) / fr[:, None], "e4m3")
    wcp = pack_weight(n((R, N)) * 1 / np.sqrt(R) / fr[:, None], "e2m1")
    return {
        "xt_words": xtp[0],
        "xt_scales": xtp[1],
        "wa_words": wap[0],
        "wa_scales": wap[1],
        "wb_words": wbp[0],
        "wb_scales": wbp[1],
        "wc_words": wcp[0],
        "wc_scales": wcp[1],
        "offs": striped(idx),
    }


def reference(xt_words, xt_scales, wa_words, wa_scales, wb_words, wb_scales, wc_words, wc_scales, offs):
    idx = unstriped(offs)
    xtu = unpack_weight(xt_words, xt_scales, "e4m3")
    wau = unpack_weight(wa_words, wa_scales, "e2m1")
    wbu = unpack_weight(wb_words, wb_scales, "e4m3")
    wcu = unpack_weight(wc_words, wc_scales, "e2m1")
    xtidxg = xtu[:, idx]
    a = wau.T @ xtidxg
    h1 = np.maximum(a, 0.0)
    ha = h1[:, 0:0 + I]
    hb = h1[:, 512:512 + I]
    haq = mxq(ha, 0, "e4m3")
    hbq = mxq(hb, 0, "e4m3")
    p = wbu.T @ haq + wcu.T @ hbq
    y = np.tanh(0.7 * p)
    return y

@@ -1,0 +1,168 @@
+from contextlib import ExitStack
+
+import concourse.mybir as mybir
+
+K, T, J, I, R, N = 512, 2048, 1024, 512, 512, 512
+FLOPS = 2 * K * R * J + 2 * 2 * R * N * I
+
+F32 = mybir.dt.float32
+BF16 = mybir.dt.bfloat16
+I32 = mybir.dt.int32
+U32 = mybir.dt.uint32
+U16 = mybir.dt.uint16
+U8 = mybir.dt.uint8
+FP8X4 = mybir.dt.float8_e4m3fn_x4
+FP4X4 = mybir.dt.float4_e2m1fn_x4
+ACT = mybir.ActivationFunctionType
+
+P = 128
+PACK = 4
+PIECE = 256
+UNIT = 128
+
+
+def load_scale_quadrant(queue, plane, scales, q, row=0):
+    queue.dma_start(
+        out=plane[:].bitcast(I32)[32 * q + row : 32 * q + row + 4, :],
+        in_=scales[0, 4 * q : 4 * q + 4, :].bitcast(I32),
+    )
+
+
+def tile_list_halves_as_partners_kernel(
+    tc, xt_words, xt_scales, wa_words, wa_scales, wb_words, wb_scales, wc_words, wc_scales, offs, out
+):
+    nc = tc.nc
+    with ExitStack() as ctx:
+        keep = ctx.enter_context(tc.tile_pool(name="keep", bufs=1))
+        reuse = ctx.enter_context(tc.tile_pool(name="reuse", bufs=1))
+        ps1 = ctx.enter_context(tc.psum_pool(name="ps1", bufs=5))
+        ps2 = ctx.enter_context(tc.psum_pool(name="ps2", bufs=3))
+
+        offsets = keep.tile([P, J // 16], U16, name="offsets")
+        x_words = keep.tile([P, T], I32, name="x_words", align_bytes=64)
+        a_words = keep.tile([P, 2 * R], U8, name="a_words", align_bytes=64)
+        a_plane = keep.tile([P, R], U8, name="a_plane", align_bytes=64)
+        g_plane = keep.tile([P, J], U8, name="g_plane", align_bytes=64)
+        warm = keep.tile([P, 8], F32, name="warm")
+        warm_out = keep.tile([P, 8], F32, name="warm_out")
+
+        x_plane = reuse.tile([P, T], U8, name="x_plane", align_bytes=64, offset=0)
+        a_plane_raw = reuse.tile([P, R], U8, name="a_plane_raw", align_bytes=64, offset=2048)
+        a_words_raw = reuse.tile([P, 2 * R], U8, name="a_words_raw", align_bytes=64, offset=4096 + 1792)
+
+        nc.vector.memset(x_plane[:].bitcast(I32), 0)
+        nc.vector.memset(a_plane_raw[:].bitcast(I32), 0)
+        nc.vector.memset(warm[:], 0.0)
+
+        nc.sync.dma_start(offsets[:], offs)
+        nc.sync.dma_start(out=a_words_raw[:].bitcast(I32), in_=wa_words[0].bitcast(I32))
+        nc.sync.dma_start(out=x_words[:], in_=xt_words[0].rearrange("p n t -> p (n t)").bitcast(I32))
+        for q in range(4):
+            load_scale_quadrant(nc.scalar, x_plane, xt_scales, q)
+        for q in range(4):
+            load_scale_quadrant(nc.scalar if q < 3 else nc.gpsimd, a_plane_raw, wa_scales, q)
+        nc.scalar.activation(out=warm_out[:], in_=warm[:], func=ACT.Tanh)
+
+        nc.vector.tensor_copy(
+            out=a_words[:].bitcast(U16).rearrange("p (t b m) -> p b t m", t=PACK, m=8),
+            in_=a_words_raw[:].bitcast(U16).rearrange("p (b m t) -> p b t m", t=PACK, m=8),
+        )
+
+        b_words = reuse.tile([P, N], I32, name="b_words", align_bytes=64, offset=4096)
+        bc_plane = reuse.tile([P, N], U8, name="bc_plane", align_bytes=64, offset=4096 + 2048)
+        c_words = reuse.tile([P, 2 * N], U8, name="c_words", align_bytes=64, offset=4096 + 2560)
+        nc.vector.memset(bc_plane[:].bitcast(I32), 0)
+        nc.sync.dma_start(out=b_words[:], in_=wb_words[0].rearrange("p n t -> p (n t)").bitcast(I32))
+        nc.sync.dma_start(out=c_words[:].bitcast(I32), in_=wc_words[0].bitcast(I32))
+        for q in range(4):
+            load_scale_quadrant(nc.sync, bc_plane, wb_scales, q, row=4)
+        for q in range(4):
+            load_scale_quadrant(nc.sync, bc_plane, wc_scales, q)
+
+        nc.vector.tensor_copy(g_plane[:], x_plane[:].indirect(offsets[:]))
+        nc.vector.tensor_copy(
+            out=a_plane[:].rearrange("p (t b m) -> p b t m", t=PACK, m=16),
+            in_=a_plane_raw[:].rearrange("p (b m t) -> p b t m", t=PACK, m=16),
+        )
+        g_words = reuse.tile([P, J], U32, name="g_words", align_bytes=64, offset=0)
+        for g in (0, 2, 1, 3):
+            nc.vector.tensor_copy(
+                g_words[:, g * PIECE : (g + 1) * PIECE],
+                x_words[:].bitcast(U32).indirect(offsets[:, g * PIECE // 16 : (g + 1) * PIECE // 16]),
+            )
+
+        codes = keep.tile([P, J], U32, name="codes", align_bytes=64)
+        scales = keep.tile([P, J], U8, name="scales", align_bytes=64)
+        hidden = {}
+
+        def first_layer(j0, on_vector):
+            acc = ps1.tile([P, PACK, UNIT], F32, name="acc1")
+            for t in range(PACK):
+                nc.tensor.matmul_mx(
+                    out=acc[:, t, :],
+                    lhsT=a_words[:, 2 * P * t : 2 * P * (t + 1)].bitcast(FP4X4),
+                    lhsT_scale=a_plane[:, P * t : P * (t + 1)],
+                    rhs=g_words[:, j0 : j0 + UNIT].bitcast(FP8X4),
+                    rhs_scale=g_plane[:, j0 : j0 + UNIT],
+                    start=True,
+                    stop=True,
+                )
+            h = keep.tile([P, UNIT, PACK], BF16, name="h%d" % j0, align_bytes=64)
+            if on_vector:
+                nc.vector.tensor_scalar_max(h[:], acc[:].rearrange("p t j -> p j t"), 0.0)
+            else:
+                nc.scalar.activation(out=h[:], in_=acc[:].rearrange("p t j -> p j t"), func=ACT.Relu)
+            hidden[j0] = h
+
+        def quantise(j0):
+            nc.vector.quantize_mx(
+                out=codes[:, j0 : j0 + UNIT].bitcast(FP8X4),
+                scales=scales[:, j0 : j0 + UNIT],
+                in_=hidden[j0][:].rearrange("p j t -> p (j t)"),
+            )
+
+        def second_layer(i0, m0, count):
+            acc = ps2.tile([P, count, PIECE], F32, name="acc2")
+            for m in range(count):
+                n0 = P * (m0 + m)
+                nc.tensor.matmul_mx(
+                    out=acc[:, m, :],
+                    lhsT=b_words[:, n0 : n0 + P].bitcast(FP8X4),
+                    lhsT_scale=bc_plane[4:P, n0 : n0 + P],
+                    rhs=codes[:, i0 : i0 + PIECE].bitcast(FP8X4),
+                    rhs_scale=scales[:, i0 : i0 + PIECE],
+                    start=(m == 0),
+                    stop=False,
+                )
+            for c in range(0, PIECE, UNIT):
+                for m in range(count):
+                    n0 = P * (m0 + m)
+                    j0 = I + i0 + c
+                    nc.tensor.matmul_mx(
+                        out=acc[:, m, c : c + UNIT],
+                        lhsT=c_words[:, 2 * n0 : 2 * (n0 + P)].bitcast(FP4X4),
+                        lhsT_scale=bc_plane[:, n0 : n0 + P],
+                        rhs=codes[:, j0 : j0 + UNIT].bitcast(FP8X4),
+                        rhs_scale=scales[:, j0 : j0 + UNIT],
+                        start=False,
+                        stop=(c == PIECE - UNIT and m == count - 1),
+                    )
+            y = keep.tile([P, count, PIECE], F32, name="y%d_%d" % (i0, m0))
+            nc.scalar.activation(out=y[:], in_=acc[:], func=ACT.Tanh, scale=0.7)
+            nc.sync.dma_start(
+                out=out.rearrange("(m p) i -> p m i", p=P)[:, m0 : m0 + count, i0 : i0 + PIECE], in_=y[:]
+            )
+
+        slots = [0, 128, 512, 640, 256, 384, 768, 896]
+        on_vector = {256, 768}
+        for n, j0 in enumerate(slots):
+            first_layer(j0, j0 in on_vector)
+            if n >= 2:
+                quantise(slots[n - 2])
+        quantise(slots[-2])
+        quantise(slots[-1])
+        second_layer(0, 0, 2)
+        second_layer(0, 2, 2)
+        second_layer(PIECE, 0, 2)
+        second_layer(PIECE, 2, 1)
+        second_layer(PIECE, 3, 1)

@@ -28,6 +28,12 @@ def load_scale_quadrant(queue, plane, scales, q, row=0):
     )
 
 
+def spread_scale_rows(queue, plane):
+    rows = plane[:].bitcast(I32)
+    for q in range(1, 4):
+        queue.dma_start(out=rows[32 * q : 32 * q + 4, :], in_=rows[4 * q : 4 * q + 4, :])
+
+
 def tile_list_halves_as_partners_kernel(
     tc, xt_words, xt_scales, wa_words, wa_scales, wb_words, wb_scales, wc_words, wc_scales, offs, out
 ):
@@ -35,60 +41,69 @@ def tile_list_halves_as_partners_kernel(
     with ExitStack() as ctx:
         keep = ctx.enter_context(tc.tile_pool(name="keep", bufs=1))
         reuse = ctx.enter_context(tc.tile_pool(name="reuse", bufs=1))
-        ps1 = ctx.enter_context(tc.psum_pool(name="ps1", bufs=5))
-        ps2 = ctx.enter_context(tc.psum_pool(name="ps2", bufs=3))
+        psum = ctx.enter_context(tc.psum_pool(name="psum", bufs=8))
 
         offsets = keep.tile([P, J // 16], U16, name="offsets")
-        x_words = keep.tile([P, T], I32, name="x_words", align_bytes=64)
-        a_words = keep.tile([P, 2 * R], U8, name="a_words", align_bytes=64)
         a_plane = keep.tile([P, R], U8, name="a_plane", align_bytes=64)
-        g_plane = keep.tile([P, J], U8, name="g_plane", align_bytes=64)
-        warm = keep.tile([P, 8], F32, name="warm")
-        warm_out = keep.tile([P, 8], F32, name="warm_out")
+        warm = keep.tile([P, 1], F32, name="warm")
+        zero_bias = keep.tile([P, 1], F32, name="zero_bias")
 
-        x_plane = reuse.tile([P, T], U8, name="x_plane", align_bytes=64, offset=0)
-        a_plane_raw = reuse.tile([P, R], U8, name="a_plane_raw", align_bytes=64, offset=2048)
-        a_words_raw = reuse.tile([P, 2 * R], U8, name="a_words_raw", align_bytes=64, offset=4096 + 1792)
+        bc_plane = keep.tile([P, 2 * N], U8, name="bc_plane", align_bytes=64)
+        x_plane = keep.tile([P, T], U8, name="x_plane", align_bytes=64)
+        g_words = keep.tile([P, J], U32, name="g_words", align_bytes=64)
+        a_plane_raw = reuse.tile([P, R], U8, name="a_plane_raw", align_bytes=64, offset=0)
+        a_words_raw = reuse.tile([P, 2 * R], U8, name="a_words_raw", align_bytes=64, offset=1024 + 1920)
+        zeros = reuse.tile([P, 1], I32, name="zeros", align_bytes=64, offset=5120)
 
-        nc.vector.memset(x_plane[:].bitcast(I32), 0)
         nc.vector.memset(a_plane_raw[:].bitcast(I32), 0)
+        nc.vector.memset(x_plane[:].bitcast(I32), 0)
+        nc.vector.memset(zeros[:], 0)
+        nc.vector.tensor_copy(bc_plane[:].bitcast(I32), zeros[:].to_broadcast([P, 2 * N // 4]))
         nc.vector.memset(warm[:], 0.0)
 
         nc.sync.dma_start(offsets[:], offs)
         nc.sync.dma_start(out=a_words_raw[:].bitcast(I32), in_=wa_words[0].bitcast(I32))
+        nc.scalar.dma_start(out=a_plane_raw[:].bitcast(I32)[0:16, :], in_=wa_scales[0].bitcast(I32))
+        for q in range(4):
+            load_scale_quadrant(nc.sync if q < 2 else nc.scalar, x_plane, xt_scales, q)
+        x_words = reuse.tile([P, T], I32, name="x_words", align_bytes=64, offset=5120)
         nc.sync.dma_start(out=x_words[:], in_=xt_words[0].rearrange("p n t -> p (n t)").bitcast(I32))
-        for q in range(4):
-            load_scale_quadrant(nc.scalar, x_plane, xt_scales, q)
-        for q in range(4):
-            load_scale_quadrant(nc.scalar if q < 3 else nc.gpsimd, a_plane_raw, wa_scales, q)
-        nc.scalar.activation(out=warm_out[:], in_=warm[:], func=ACT.Tanh)
+        nc.sync.dma_start(out=bc_plane[:, 0:N].bitcast(I32)[0:16, :], in_=wb_scales[0].bitcast(I32))
+        nc.sync.dma_start(out=bc_plane[:, N : 2 * N].bitcast(I32)[0:16, :], in_=wc_scales[0].bitcast(I32))
+        nc.scalar.activation(out=zero_bias[:], in_=warm[:], func=ACT.Tanh)
 
+        nc.vector.tensor_copy(
+            out=a_plane[:].rearrange("p (t b m) -> p b t m", t=PACK, m=16),
+            in_=a_plane_raw[:].rearrange("p (b m t) -> p b t m", t=PACK, m=16),
+        )
+        spread_scale_rows(nc.scalar, a_plane)
+        a_words = reuse.tile([P, 2 * R], U8, name="a_words", align_bytes=64, offset=0)
         nc.vector.tensor_copy(
             out=a_words[:].bitcast(U16).rearrange("p (t b m) -> p b t m", t=PACK, m=8),
             in_=a_words_raw[:].bitcast(U16).rearrange("p (b m t) -> p b t m", t=PACK, m=8),
         )
 
-        b_words = reuse.tile([P, N], I32, name="b_words", align_bytes=64, offset=4096)
-        bc_plane = reuse.tile([P, N], U8, name="bc_plane", align_bytes=64, offset=4096 + 2048)
-        c_words = reuse.tile([P, 2 * N], U8, name="c_words", align_bytes=64, offset=4096 + 2560)
-        nc.vector.memset(bc_plane[:].bitcast(I32), 0)
+        b_words = reuse.tile([P, N], I32, name="b_words", align_bytes=64, offset=1024)
+        c_words = reuse.tile([P, 2 * N], U8, name="c_words", align_bytes=64, offset=1024 + 2048 + 768)
         nc.sync.dma_start(out=b_words[:], in_=wb_words[0].rearrange("p n t -> p (n t)").bitcast(I32))
         nc.sync.dma_start(out=c_words[:].bitcast(I32), in_=wc_words[0].bitcast(I32))
-        for q in range(4):
-            load_scale_quadrant(nc.sync, bc_plane, wb_scales, q, row=4)
-        for q in range(4):
-            load_scale_quadrant(nc.sync, bc_plane, wc_scales, q)
+        spread_scale_rows(nc.sync, bc_plane)
 
-        nc.vector.tensor_copy(g_plane[:], x_plane[:].indirect(offsets[:]))
-        nc.vector.tensor_copy(
-            out=a_plane[:].rearrange("p (t b m) -> p b t m", t=PACK, m=16),
-            in_=a_plane_raw[:].rearrange("p (b m t) -> p b t m", t=PACK, m=16),
-        )
-        g_words = reuse.tile([P, J], U32, name="g_words", align_bytes=64, offset=0)
+        g_plane = {}
+
+        def piece_offsets(g):
+            return offsets[:, g * PIECE // 16 : (g + 1) * PIECE // 16]
+
+        def gather_plane(g, slot):
+            g_plane[g] = reuse.tile([P, PIECE], U8, name="g_plane%d" % g, align_bytes=64, offset=1024 + 2048 + slot * PIECE)
+            nc.vector.tensor_copy(g_plane[g][:], x_plane[:].indirect(piece_offsets(g)))
+
+        gather_plane(0, 0)
+        gather_plane(2, 1)
+        gather_plane(1, 2)
         for g in (0, 2, 1, 3):
             nc.vector.tensor_copy(
-                g_words[:, g * PIECE : (g + 1) * PIECE],
-                x_words[:].bitcast(U32).indirect(offsets[:, g * PIECE // 16 : (g + 1) * PIECE // 16]),
+                g_words[:, g * PIECE : (g + 1) * PIECE], x_words[:].bitcast(U32).indirect(piece_offsets(g))
             )
 
         codes = keep.tile([P, J], U32, name="codes", align_bytes=64)
@@ -96,14 +111,14 @@ def tile_list_halves_as_partners_kernel(
         hidden = {}
 
         def first_layer(j0, on_vector):
-            acc = ps1.tile([P, PACK, UNIT], F32, name="acc1")
+            acc = psum.tile([P, PACK, UNIT], F32, name="acc")
             for t in range(PACK):
                 nc.tensor.matmul_mx(
                     out=acc[:, t, :],
                     lhsT=a_words[:, 2 * P * t : 2 * P * (t + 1)].bitcast(FP4X4),
                     lhsT_scale=a_plane[:, P * t : P * (t + 1)],
                     rhs=g_words[:, j0 : j0 + UNIT].bitcast(FP8X4),
-                    rhs_scale=g_plane[:, j0 : j0 + UNIT],
+                    rhs_scale=g_plane[j0 // PIECE][:, j0 % PIECE : j0 % PIECE + UNIT],
                     start=True,
                     stop=True,
                 )
@@ -122,13 +137,13 @@ def tile_list_halves_as_partners_kernel(
             )
 
         def second_layer(i0, m0, count):
-            acc = ps2.tile([P, count, PIECE], F32, name="acc2")
+            acc = psum.tile([P, count, PIECE], F32, name="acc")
             for m in range(count):
                 n0 = P * (m0 + m)
                 nc.tensor.matmul_mx(
                     out=acc[:, m, :],
                     lhsT=b_words[:, n0 : n0 + P].bitcast(FP8X4),
-                    lhsT_scale=bc_plane[4:P, n0 : n0 + P],
+                    lhsT_scale=bc_plane[:, n0 : n0 + P],
                     rhs=codes[:, i0 : i0 + PIECE].bitcast(FP8X4),
                     rhs_scale=scales[:, i0 : i0 + PIECE],
                     start=(m == 0),
@@ -141,14 +156,14 @@ def tile_list_halves_as_partners_kernel(
                     nc.tensor.matmul_mx(
                         out=acc[:, m, c : c + UNIT],
                         lhsT=c_words[:, 2 * n0 : 2 * (n0 + P)].bitcast(FP4X4),
-                        lhsT_scale=bc_plane[:, n0 : n0 + P],
+                        lhsT_scale=bc_plane[:, N + n0 : N + n0 + P],
                         rhs=codes[:, j0 : j0 + UNIT].bitcast(FP8X4),
                         rhs_scale=scales[:, j0 : j0 + UNIT],
                         start=False,
                         stop=(c == PIECE - UNIT and m == count - 1),
                     )
             y = keep.tile([P, count, PIECE], F32, name="y%d_%d" % (i0, m0))
-            nc.scalar.activation(out=y[:], in_=acc[:], func=ACT.Tanh, scale=0.7)
+            nc.scalar.activation(out=y[:], in_=acc[:], func=ACT.Tanh, bias=zero_bias[:], scale=0.7)
             nc.sync.dma_start(
                 out=out.rearrange("(m p) i -> p m i", p=P)[:, m0 : m0 + count, i0 : i0 + PIECE], in_=y[:]
             )
@@ -157,6 +172,8 @@ def tile_list_halves_as_partners_kernel(
         on_vector = {256, 768}
         for n, j0 in enumerate(slots):
             first_layer(j0, j0 in on_vector)
+            if n == 1:
+                gather_plane(3, 0)
             if n >= 2:
                 quantise(slots[n - 2])
         quantise(slots[-2])

@@ -17,21 +17,36 @@ ACT = mybir.ActivationFunctionType
 
 P = 128
 PACK = 4
+QUADRANT = 32
+BLOCKS = 16
+LIST_ROWS = 16
+BANKS = 8
 PIECE = 256
 UNIT = 128
+LINE = 16
+
+A_WORDS_AT = 0
+A_PLANE_RAW_AT = A_WORDS_AT
+B_WORDS_AT = A_WORDS_AT + 2 * R
+G_PLANE_AT = B_WORDS_AT + 4 * N
+G_PLANE_PLACES = 3
+C_WORDS_AT = G_PLANE_AT + G_PLANE_PLACES * PIECE
+A_WORDS_RAW_AT = G_PLANE_AT - (2 * R - G_PLANE_PLACES * PIECE) // 2
+X_WORDS_AT = 5 * 1024
+ZEROS_AT = X_WORDS_AT
 
 
-def load_scale_quadrant(queue, plane, scales, q, row=0):
+def load_scale_quadrant(queue, plane, scales, q):
     queue.dma_start(
-        out=plane[:].bitcast(I32)[32 * q + row : 32 * q + row + 4, :],
+        out=plane[:].bitcast(I32)[QUADRANT * q : QUADRANT * q + 4, :],
         in_=scales[0, 4 * q : 4 * q + 4, :].bitcast(I32),
     )
 
 
 def spread_scale_rows(queue, plane):
     rows = plane[:].bitcast(I32)
-    for q in range(1, 4):
-        queue.dma_start(out=rows[32 * q : 32 * q + 4, :], in_=rows[4 * q : 4 * q + 4, :])
+    for q in range(1, P // QUADRANT):
+        queue.dma_start(out=rows[QUADRANT * q : QUADRANT * q + 4, :], in_=rows[4 * q : 4 * q + 4, :])
 
 
 def tile_list_halves_as_partners_kernel(
@@ -41,9 +56,9 @@ def tile_list_halves_as_partners_kernel(
     with ExitStack() as ctx:
         keep = ctx.enter_context(tc.tile_pool(name="keep", bufs=1))
         reuse = ctx.enter_context(tc.tile_pool(name="reuse", bufs=1))
-        psum = ctx.enter_context(tc.psum_pool(name="psum", bufs=8))
+        psum = ctx.enter_context(tc.psum_pool(name="psum", bufs=BANKS))
 
-        offsets = keep.tile([P, J // 16], U16, name="offsets")
+        offsets = keep.tile([P, J // LIST_ROWS], U16, name="offsets")
         a_plane = keep.tile([P, R], U8, name="a_plane", align_bytes=64)
         warm = keep.tile([P, 1], F32, name="warm")
         zero_bias = keep.tile([P, 1], F32, name="zero_bias")
@@ -51,9 +66,9 @@ def tile_list_halves_as_partners_kernel(
         bc_plane = keep.tile([P, 2 * N], U8, name="bc_plane", align_bytes=64)
         x_plane = keep.tile([P, T], U8, name="x_plane", align_bytes=64)
         g_words = keep.tile([P, J], U32, name="g_words", align_bytes=64)
-        a_plane_raw = reuse.tile([P, R], U8, name="a_plane_raw", align_bytes=64, offset=0)
-        a_words_raw = reuse.tile([P, 2 * R], U8, name="a_words_raw", align_bytes=64, offset=1024 + 1920)
-        zeros = reuse.tile([P, 1], I32, name="zeros", align_bytes=64, offset=5120)
+        a_plane_raw = reuse.tile([P, R], U8, name="a_plane_raw", align_bytes=64, offset=A_PLANE_RAW_AT)
+        a_words_raw = reuse.tile([P, 2 * R], U8, name="a_words_raw", align_bytes=64, offset=A_WORDS_RAW_AT)
+        zeros = reuse.tile([P, 1], I32, name="zeros", align_bytes=64, offset=ZEROS_AT)
 
         nc.vector.memset(a_plane_raw[:].bitcast(I32), 0)
         nc.vector.memset(x_plane[:].bitcast(I32), 0)
@@ -63,45 +78,48 @@ def tile_list_halves_as_partners_kernel(
 
         nc.sync.dma_start(offsets[:], offs)
         nc.sync.dma_start(out=a_words_raw[:].bitcast(I32), in_=wa_words[0].bitcast(I32))
-        nc.scalar.dma_start(out=a_plane_raw[:].bitcast(I32)[0:16, :], in_=wa_scales[0].bitcast(I32))
-        for q in range(4):
-            load_scale_quadrant(nc.sync if q < 2 else nc.scalar, x_plane, xt_scales, q)
-        x_words = reuse.tile([P, T], I32, name="x_words", align_bytes=64, offset=5120)
+        nc.scalar.dma_start(out=a_plane_raw[:].bitcast(I32)[0:BLOCKS, :], in_=wa_scales[0].bitcast(I32))
+        for q in range(P // QUADRANT):
+            load_scale_quadrant(nc.sync, x_plane, xt_scales, q)
+        x_words = reuse.tile([P, T], I32, name="x_words", align_bytes=64, offset=X_WORDS_AT)
         nc.sync.dma_start(out=x_words[:], in_=xt_words[0].rearrange("p n t -> p (n t)").bitcast(I32))
-        nc.sync.dma_start(out=bc_plane[:, 0:N].bitcast(I32)[0:16, :], in_=wb_scales[0].bitcast(I32))
-        nc.sync.dma_start(out=bc_plane[:, N : 2 * N].bitcast(I32)[0:16, :], in_=wc_scales[0].bitcast(I32))
+        nc.sync.dma_start(out=bc_plane[:, 0:N].bitcast(I32)[0:BLOCKS, :], in_=wb_scales[0].bitcast(I32))
+        nc.sync.dma_start(out=bc_plane[:, N : 2 * N].bitcast(I32)[0:BLOCKS, :], in_=wc_scales[0].bitcast(I32))
+
         nc.scalar.activation(out=zero_bias[:], in_=warm[:], func=ACT.Tanh)
 
         nc.vector.tensor_copy(
-            out=a_plane[:].rearrange("p (t b m) -> p b t m", t=PACK, m=16),
-            in_=a_plane_raw[:].rearrange("p (b m t) -> p b t m", t=PACK, m=16),
+            out=a_plane[:].rearrange("p (t b m) -> p b t m", t=PACK, m=LINE),
+            in_=a_plane_raw[:].rearrange("p (b m t) -> p b t m", t=PACK, m=LINE),
         )
         spread_scale_rows(nc.scalar, a_plane)
-        a_words = reuse.tile([P, 2 * R], U8, name="a_words", align_bytes=64, offset=0)
+        a_words = reuse.tile([P, 2 * R], U8, name="a_words", align_bytes=64, offset=A_WORDS_AT)
         nc.vector.tensor_copy(
-            out=a_words[:].bitcast(U16).rearrange("p (t b m) -> p b t m", t=PACK, m=8),
-            in_=a_words_raw[:].bitcast(U16).rearrange("p (b m t) -> p b t m", t=PACK, m=8),
+            out=a_words[:].bitcast(U16).rearrange("p (t b m) -> p b t m", t=PACK, m=LINE // 2),
+            in_=a_words_raw[:].bitcast(U16).rearrange("p (b m t) -> p b t m", t=PACK, m=LINE // 2),
         )
 
-        b_words = reuse.tile([P, N], I32, name="b_words", align_bytes=64, offset=1024)
-        c_words = reuse.tile([P, 2 * N], U8, name="c_words", align_bytes=64, offset=1024 + 2048 + 768)
+        b_words = reuse.tile([P, N], I32, name="b_words", align_bytes=64, offset=B_WORDS_AT)
+        c_words = reuse.tile([P, 2 * N], U8, name="c_words", align_bytes=64, offset=C_WORDS_AT)
         nc.sync.dma_start(out=b_words[:], in_=wb_words[0].rearrange("p n t -> p (n t)").bitcast(I32))
         nc.sync.dma_start(out=c_words[:].bitcast(I32), in_=wc_words[0].bitcast(I32))
         spread_scale_rows(nc.sync, bc_plane)
 
+        pieces = [g + half * (I // PIECE) for g in range(I // PIECE) for half in range(2)]
         g_plane = {}
 
         def piece_offsets(g):
-            return offsets[:, g * PIECE // 16 : (g + 1) * PIECE // 16]
+            return offsets[:, g * PIECE // LIST_ROWS : (g + 1) * PIECE // LIST_ROWS]
 
-        def gather_plane(g, slot):
-            g_plane[g] = reuse.tile([P, PIECE], U8, name="g_plane%d" % g, align_bytes=64, offset=1024 + 2048 + slot * PIECE)
+        def gather_plane(g, place):
+            g_plane[g] = reuse.tile(
+                [P, PIECE], U8, name="g_plane%d" % g, align_bytes=64, offset=G_PLANE_AT + place * PIECE
+            )
             nc.vector.tensor_copy(g_plane[g][:], x_plane[:].indirect(piece_offsets(g)))
 
-        gather_plane(0, 0)
-        gather_plane(2, 1)
-        gather_plane(1, 2)
-        for g in (0, 2, 1, 3):
+        for place in range(G_PLANE_PLACES):
+            gather_plane(pieces[place], place)
+        for g in pieces:
             nc.vector.tensor_copy(
                 g_words[:, g * PIECE : (g + 1) * PIECE], x_words[:].bitcast(U32).indirect(piece_offsets(g))
             )
@@ -168,16 +186,19 @@ def tile_list_halves_as_partners_kernel(
                 out=out.rearrange("(m p) i -> p m i", p=P)[:, m0 : m0 + count, i0 : i0 + PIECE], in_=y[:]
             )
 
-        slots = [0, 128, 512, 640, 256, 384, 768, 896]
-        on_vector = {256, 768}
-        for n, j0 in enumerate(slots):
-            first_layer(j0, j0 in on_vector)
-            if n == 1:
-                gather_plane(3, 0)
-            if n >= 2:
-                quantise(slots[n - 2])
-        quantise(slots[-2])
-        quantise(slots[-1])
+        starts = [g * PIECE + c for g in pieces for c in range(0, PIECE, UNIT)]
+        vector_banks = [g * PIECE for g in pieces[2:]]
+        banks_a_piece = PIECE // UNIT
+        lag = 2
+        for n, j0 in enumerate(starts):
+            first_layer(j0, j0 in vector_banks)
+            if n == banks_a_piece - 1:
+                gather_plane(pieces[-1], 0)
+            if n >= lag:
+                quantise(starts[n - lag])
+        for j0 in starts[-lag:]:
+            quantise(j0)
+
         second_layer(0, 0, 2)
         second_layer(0, 2, 2)
         second_layer(PIECE, 0, 2)

from contextlib import ExitStack

import concourse.mybir as mybir

K, T, J, I, R, N = 512, 2048, 1024, 512, 512, 512
FLOPS = 2 * K * R * J + 2 * 2 * R * N * I

F32 = mybir.dt.float32
BF16 = mybir.dt.bfloat16
I32 = mybir.dt.int32
U32 = mybir.dt.uint32
U16 = mybir.dt.uint16
U8 = mybir.dt.uint8
FP8X4 = mybir.dt.float8_e4m3fn_x4
FP4X4 = mybir.dt.float4_e2m1fn_x4
ACT = mybir.ActivationFunctionType

P = 128
PACK = 4
QUADRANT = 32
BLOCKS = 16
LIST_ROWS = 16
BANKS = 8
PIECE = 256
UNIT = 128
LINE = 16

A_WORDS_AT = 0
A_PLANE_RAW_AT = A_WORDS_AT
B_WORDS_AT = A_WORDS_AT + 2 * R
G_PLANE_AT = B_WORDS_AT + 4 * N
G_PLANE_PLACES = 3
C_WORDS_AT = G_PLANE_AT + G_PLANE_PLACES * PIECE
A_WORDS_RAW_AT = G_PLANE_AT - (2 * R - G_PLANE_PLACES * PIECE) // 2
X_WORDS_AT = 5 * 1024
ZEROS_AT = X_WORDS_AT


def load_scale_quadrant(queue, plane, scales, q):
    queue.dma_start(
        out=plane[:].bitcast(I32)[QUADRANT * q : QUADRANT * q + 4, :],
        in_=scales[0, 4 * q : 4 * q + 4, :].bitcast(I32),
    )


def spread_scale_rows(queue, plane):
    rows = plane[:].bitcast(I32)
    for q in range(1, P // QUADRANT):
        queue.dma_start(out=rows[QUADRANT * q : QUADRANT * q + 4, :], in_=rows[4 * q : 4 * q + 4, :])


def tile_list_halves_as_partners_kernel(
    tc, xt_words, xt_scales, wa_words, wa_scales, wb_words, wb_scales, wc_words, wc_scales, offs, out
):
    nc = tc.nc
    with ExitStack() as ctx:
        keep = ctx.enter_context(tc.tile_pool(name="keep", bufs=1))
        reuse = ctx.enter_context(tc.tile_pool(name="reuse", bufs=1))
        psum = ctx.enter_context(tc.psum_pool(name="psum", bufs=BANKS))

        offsets = keep.tile([P, J // LIST_ROWS], U16, name="offsets")
        a_plane = keep.tile([P, R], U8, name="a_plane", align_bytes=64)
        warm = keep.tile([P, 1], F32, name="warm")
        zero_bias = keep.tile([P, 1], F32, name="zero_bias")

        bc_plane = keep.tile([P, 2 * N], U8, name="bc_plane", align_bytes=64)
        x_plane = keep.tile([P, T], U8, name="x_plane", align_bytes=64)
        g_words = keep.tile([P, J], U32, name="g_words", align_bytes=64)
        a_plane_raw = reuse.tile([P, R], U8, name="a_plane_raw", align_bytes=64, offset=A_PLANE_RAW_AT)
        a_words_raw = reuse.tile([P, 2 * R], U8, name="a_words_raw", align_bytes=64, offset=A_WORDS_RAW_AT)
        zeros = reuse.tile([P, 1], I32, name="zeros", align_bytes=64, offset=ZEROS_AT)

        nc.vector.memset(a_plane_raw[:].bitcast(I32), 0)
        nc.vector.memset(x_plane[:].bitcast(I32), 0)
        nc.vector.memset(zeros[:], 0)
        nc.vector.tensor_copy(bc_plane[:].bitcast(I32), zeros[:].to_broadcast([P, 2 * N // 4]))
        nc.vector.memset(warm[:], 0.0)

        nc.sync.dma_start(offsets[:], offs)
        nc.sync.dma_start(out=a_words_raw[:].bitcast(I32), in_=wa_words[0].bitcast(I32))
        nc.scalar.dma_start(out=a_plane_raw[:].bitcast(I32)[0:BLOCKS, :], in_=wa_scales[0].bitcast(I32))
        for q in range(P // QUADRANT):
            load_scale_quadrant(nc.sync, x_plane, xt_scales, q)
        x_words = reuse.tile([P, T], I32, name="x_words", align_bytes=64, offset=X_WORDS_AT)
        nc.sync.dma_start(out=x_words[:], in_=xt_words[0].rearrange("p n t -> p (n t)").bitcast(I32))
        nc.sync.dma_start(out=bc_plane[:, 0:N].bitcast(I32)[0:BLOCKS, :], in_=wb_scales[0].bitcast(I32))
        nc.sync.dma_start(out=bc_plane[:, N : 2 * N].bitcast(I32)[0:BLOCKS, :], in_=wc_scales[0].bitcast(I32))

        nc.scalar.activation(out=zero_bias[:], in_=warm[:], func=ACT.Tanh)

        nc.vector.tensor_copy(
            out=a_plane[:].rearrange("p (t b m) -> p b t m", t=PACK, m=LINE),
            in_=a_plane_raw[:].rearrange("p (b m t) -> p b t m", t=PACK, m=LINE),
        )
        spread_scale_rows(nc.scalar, a_plane)
        a_words = reuse.tile([P, 2 * R], U8, name="a_words", align_bytes=64, offset=A_WORDS_AT)
        nc.vector.tensor_copy(
            out=a_words[:].bitcast(U16).rearrange("p (t b m) -> p b t m", t=PACK, m=LINE // 2),
            in_=a_words_raw[:].bitcast(U16).rearrange("p (b m t) -> p b t m", t=PACK, m=LINE // 2),
        )

        b_words = reuse.tile([P, N], I32, name="b_words", align_bytes=64, offset=B_WORDS_AT)
        c_words = reuse.tile([P, 2 * N], U8, name="c_words", align_bytes=64, offset=C_WORDS_AT)
        nc.sync.dma_start(out=b_words[:], in_=wb_words[0].rearrange("p n t -> p (n t)").bitcast(I32))
        nc.sync.dma_start(out=c_words[:].bitcast(I32), in_=wc_words[0].bitcast(I32))
        spread_scale_rows(nc.sync, bc_plane)

        pieces = [g + half * (I // PIECE) for g in range(I // PIECE) for half in range(2)]
        g_plane = {}

        def piece_offsets(g):
            return offsets[:, g * PIECE // LIST_ROWS : (g + 1) * PIECE // LIST_ROWS]

        def gather_plane(g, place):
            g_plane[g] = reuse.tile(
                [P, PIECE], U8, name="g_plane%d" % g, align_bytes=64, offset=G_PLANE_AT + place * PIECE
            )
            nc.vector.tensor_copy(g_plane[g][:], x_plane[:].indirect(piece_offsets(g)))

        for place in range(G_PLANE_PLACES):
            gather_plane(pieces[place], place)
        for g in pieces:
            nc.vector.tensor_copy(
                g_words[:, g * PIECE : (g + 1) * PIECE], x_words[:].bitcast(U32).indirect(piece_offsets(g))
            )

        codes = keep.tile([P, J], U32, name="codes", align_bytes=64)
        scales = keep.tile([P, J], U8, name="scales", align_bytes=64)
        hidden = {}

        def first_layer(j0, on_vector):
            acc = psum.tile([P, PACK, UNIT], F32, name="acc")
            for t in range(PACK):
                nc.tensor.matmul_mx(
                    out=acc[:, t, :],
                    lhsT=a_words[:, 2 * P * t : 2 * P * (t + 1)].bitcast(FP4X4),
                    lhsT_scale=a_plane[:, P * t : P * (t + 1)],
                    rhs=g_words[:, j0 : j0 + UNIT].bitcast(FP8X4),
                    rhs_scale=g_plane[j0 // PIECE][:, j0 % PIECE : j0 % PIECE + UNIT],
                    start=True,
                    stop=True,
                )
            h = keep.tile([P, UNIT, PACK], BF16, name="h%d" % j0, align_bytes=64)
            if on_vector:
                nc.vector.tensor_scalar_max(h[:], acc[:].rearrange("p t j -> p j t"), 0.0)
            else:
                nc.scalar.activation(out=h[:], in_=acc[:].rearrange("p t j -> p j t"), func=ACT.Relu)
            hidden[j0] = h

        def quantise(j0):
            nc.vector.quantize_mx(
                out=codes[:, j0 : j0 + UNIT].bitcast(FP8X4),
                scales=scales[:, j0 : j0 + UNIT],
                in_=hidden[j0][:].rearrange("p j t -> p (j t)"),
            )

        def second_layer(i0, m0, count):
            acc = psum.tile([P, count, PIECE], F32, name="acc")
            for m in range(count):
                n0 = P * (m0 + m)
                nc.tensor.matmul_mx(
                    out=acc[:, m, :],
                    lhsT=b_words[:, n0 : n0 + P].bitcast(FP8X4),
                    lhsT_scale=bc_plane[:, n0 : n0 + P],
                    rhs=codes[:, i0 : i0 + PIECE].bitcast(FP8X4),
                    rhs_scale=scales[:, i0 : i0 + PIECE],
                    start=(m == 0),
                    stop=False,
                )
            for c in range(0, PIECE, UNIT):
                for m in range(count):
                    n0 = P * (m0 + m)
                    j0 = I + i0 + c
                    nc.tensor.matmul_mx(
                        out=acc[:, m, c : c + UNIT],
                        lhsT=c_words[:, 2 * n0 : 2 * (n0 + P)].bitcast(FP4X4),
                        lhsT_scale=bc_plane[:, N + n0 : N + n0 + P],
                        rhs=codes[:, j0 : j0 + UNIT].bitcast(FP8X4),
                        rhs_scale=scales[:, j0 : j0 + UNIT],
                        start=False,
                        stop=(c == PIECE - UNIT and m == count - 1),
                    )
            y = keep.tile([P, count, PIECE], F32, name="y%d_%d" % (i0, m0))
            nc.scalar.activation(out=y[:], in_=acc[:], func=ACT.Tanh, bias=zero_bias[:], scale=0.7)
            nc.sync.dma_start(
                out=out.rearrange("(m p) i -> p m i", p=P)[:, m0 : m0 + count, i0 : i0 + PIECE], in_=y[:]
            )

        starts = [g * PIECE + c for g in pieces for c in range(0, PIECE, UNIT)]
        vector_banks = [g * PIECE for g in pieces[2:]]
        banks_a_piece = PIECE // UNIT
        lag = 2
        for n, j0 in enumerate(starts):
            first_layer(j0, j0 in vector_banks)
            if n == banks_a_piece - 1:
                gather_plane(pieces[-1], 0)
            if n >= lag:
                quantise(starts[n - lag])
        for j0 in starts[-lag:]:
            quantise(j0)

        second_layer(0, 0, 2)
        second_layer(0, 2, 2)
        second_layer(PIECE, 0, 2)
        second_layer(PIECE, 2, 1)
        second_layer(PIECE, 3, 1)
